import numpy as np
import ml_dtypes


def mxq(x, axis, fmt="e4m3"):
    dtype, down = {"e4m3": (ml_dtypes.float8_e4m3fn, 7), "e5m2": (ml_dtypes.float8_e5m2, 14)}[fmt]
    v = np.moveaxis(np.asarray(x, np.float32).astype(ml_dtypes.bfloat16).astype(np.float64), axis, -1)
    blocks = v.reshape(v.shape[:-1] + (-1, 32))
    amax = np.abs(blocks).max(-1, keepdims=True)
    byte = np.maximum(np.where(amax > 0, np.frexp(amax)[1] - 1 + 127, 0) - down, 1)
    scale = np.exp2(byte - 127.0)
    codes = (blocks / scale).astype(np.float32).astype(dtype).astype(np.float64)
    return np.moveaxis((codes * scale).reshape(v.shape), -1, axis)


WIDE = False


def mx_kscale(k):
    if not WIDE:
        return np.ones(k)
    levels = np.array([10, -10, 5, -5, 0])
    if k % 512:
        return np.exp2(np.random.permutation(np.resize(levels, k // 32))).repeat(32)
    a = np.empty((k // 512, 16))
    for p in range(k // 512):
        a[p, :8] = np.random.permutation(np.resize(levels, 8))
        for g in range(8):
            far = levels[np.abs(levels - a[p, g]) >= 10]
            a[p, g + 8] = far[np.random.randint(len(far))]
    return np.exp2(a.ravel()).repeat(32)


def f64(x):
    return np.asarray(x).astype(np.float64)


def striped(idx):
    return np.tile(idx.reshape(-1, 16).T, (8, 1)).astype(np.uint16)


def unstriped(offs):
    return offs[:16].T.reshape(-1).astype(np.int64)


def striped8(idx):
    return np.concatenate([x.reshape(-1, 16).T for x in idx]).astype(np.uint16)


def runs(offs, k):
    lists = np.stack([offs[16 * r : 16 * r + 16].T.reshape(-1) for r in range(8)]).astype(np.int64)
    return lists[np.arange(k) % 512 // 64]


def pack_weight(w):
    k, n = w.shape
    w = f64(np.asarray(w, np.float32).astype(ml_dtypes.bfloat16)).reshape(k // 32, 32, n)
    amax = np.abs(w).max(1)
    byte = np.clip(np.where(amax > 0, np.frexp(amax)[1] - 1 + 127 - 7, 1), 1, 254)
    scaled = (w * np.exp2(127.0 - byte)[:, None, :]).reshape(k, n).astype(np.float32)
    words = np.ascontiguousarray(scaled.reshape(k // 512, 128, 4, n).transpose(0, 1, 3, 2)).astype(ml_dtypes.float8_e4m3fn).view(np.uint8)
    return words, np.ascontiguousarray(byte.astype(np.uint8).reshape(k // 512, 16, n))


def unpack_weight(words, scales):
    g, p, n, _ = words.shape
    vals = np.ascontiguousarray(words).view(ml_dtypes.float8_e4m3fn).astype(np.float64) * np.repeat(np.exp2(scales.astype(np.float64) - 127.0), 8, axis=1)[..., None]
    return vals.transpose(0, 1, 3, 2).reshape(g * 512, n)


E2M1 = np.array([0.0, 0.5, 1.0, 1.5, 2.0, 3.0, 4.0, 6.0, -0.0, -0.5, -1.0, -1.5, -2.0, -3.0, -4.0, -6.0])


def pack_fp4(w):
    k, n = w.shape
    w = f64(np.asarray(w, np.float32).astype(ml_dtypes.bfloat16)).reshape(k // 32, 32, n)
    amax = np.abs(w).max(1)
    mant, ex = np.frexp(amax / 6.0)
    byte = np.clip(np.where(amax > 0, np.where(mant > 0.5, ex, ex - 1) + 127, 1), 1, 254)
    scaled = (w * np.exp2(127.0 - byte)[:, None, :]).reshape(k, n).astype(np.float32)
    c = np.ascontiguousarray(scaled.reshape(k // 512, 128, 4, n).transpose(0, 1, 3, 2)).astype(ml_dtypes.float4_e2m1fn).view(np.uint8) & 0xF
    words = (c[..., 0::2] | (c[..., 1::2] << 4)).reshape(k // 512, 128, 2 * n)
    return np.ascontiguousarray(words), np.ascontiguousarray(byte.astype(np.uint8).reshape(k // 512, 16, n))


def unpack_fp4(words, scales):
    g, _, n = scales.shape
    words = np.ascontiguousarray(words).reshape(g, 128, n, 2)
    nib = np.empty((g, 128, n, 4), np.uint8)
    nib[..., 0::2] = words & 0xF
    nib[..., 1::2] = words >> 4
    vals = E2M1[nib] * np.repeat(np.exp2(scales.astype(np.float64) - 127.0), 8, axis=1)[..., None]
    return vals.transpose(0, 1, 3, 2).reshape(g * 512, n)


def planes(y):
    n, m = y.shape
    v = y.astype(np.float32).astype(ml_dtypes.bfloat16).astype(np.float64).reshape(n // 32, 32, m)
    top = np.abs(v).max(1)
    byte = np.clip(np.where(top > 0, np.frexp(top)[1] - 1 + 127 - 7, 1), 1, 254)
    codes = (v * np.exp2(127.0 - byte)[:, None, :]).reshape(n, m).astype(np.float32).astype(ml_dtypes.float8_e4m3fn).view(np.uint8)
    words = codes.reshape(n // 512, 128, 4, m).transpose(0, 1, 3, 2)
    return np.ascontiguousarray(words), np.ascontiguousarray(byte.astype(np.uint8).reshape(n // 512, 16, m))


K, T, S, N, H = 512, 2048, 512, 512, 512


def setup_inputs():
    n = np.random.standard_normal
    s = mx_kscale(K)[:, None]
    u = mx_kscale(S)
    packed_xT = pack_weight(n((K, T)) * s)
    packed_w1 = pack_fp4(n((S, N)) / np.sqrt(S) / u[:, None])
    return {
        "x_words": packed_xT[0],
        "x_scales": packed_xT[1],
        "wa": (n((K, H)) / np.sqrt(K) / s).astype(np.float32),
        "gt": (np.random.uniform(0.5, 1.5, (S, 1)) * u[:, None]).astype(np.float32),
        "w1_words": packed_w1[0],
        "w1_scales": packed_w1[1],
        "offs": striped(np.random.permutation(T)[:S]),
        "n1": striped8(np.stack([np.random.permutation(H) for _ in range(8)])),
        "n2": striped8(np.stack([np.random.permutation(H) for _ in range(8)])),
        "n3": striped8(np.stack([np.random.permutation(H) for _ in range(8)])),
        "n4": striped8(np.stack([np.random.permutation(H) for _ in range(8)])),
    }


def reference(x_words, x_scales, wa, gt, w1_words, w1_scales, offs, n1, n2, n3, n4):
    xq = unpack_weight(x_words, x_scales)[:, unstriped(offs)]
    y = xq.T @ mxq(f64(wa), 0, "e4m3")
    z = f64(gt) * (y[np.arange(S)[:, None], runs(n1, S)] - (y[np.arange(S)[:, None], runs(n2, S)]))
    h = unpack_fp4(w1_words, w1_scales).T @ mxq(z, 0, "e4m3")
    out_0 = (h - (h[np.arange(N)[:, None], runs(n3, N)])) / (np.abs(h[np.arange(N)[:, None], runs(n4, N)] - h) + 0.5)
    return (out_0,) + planes(out_0)

@@ -1,0 +1,194 @@
+from contextlib import ExitStack
+
+import concourse.mybir as mybir
+
+K, T, S, N, H = 512, 2048, 512, 512, 512
+FLOPS = 2 * K * S * H + 2 * S * N * H
+
+F32 = mybir.dt.float32
+BF16 = mybir.dt.bfloat16
+I32 = mybir.dt.int32
+U32 = mybir.dt.uint32
+U16 = mybir.dt.uint16
+U8 = mybir.dt.uint8
+FP8X4 = mybir.dt.float8_e4m3fn_x4
+FP4X4 = mybir.dt.float4_e2m1fn_x4
+ACT = mybir.ActivationFunctionType
+SUB = mybir.AluOpType.subtract
+MULT = mybir.AluOpType.mult
+
+P = 128
+PACK = 4
+WA_CHUNKS = (256, 256)
+Z_CHUNKS = (256, 256)
+Z_VECTOR_COLS = 160
+OUT_CHUNKS = (256, 128, 128)
+
+
+def spans(widths):
+    out, at = [], 0
+    for w in widths:
+        out.append((at, at + w))
+        at = at + w
+    return out
+
+
+def interleave(copy, dst, src):
+    copy(dst.rearrange("p (c i) t -> p c t i", i=4), src.rearrange("p t (c i) -> p c t i", i=4))
+
+
+def tile_picked_tokgapfrac_none_po_kernel(tc, x_words, x_scales, wa, gt, w1_words, w1_scales, offs, n1, n2, n3, n4, out_0, out_1, out_2):
+    nc = tc.nc
+    with ExitStack() as ctx:
+        keep = ctx.enter_context(tc.tile_pool(name="keep", bufs=1))
+        psum = ctx.enter_context(tc.psum_pool(name="psum", bufs=1))
+
+        def sb(name, shape, dtype):
+            return keep.tile(shape, dtype, name=name, align_bytes=64)
+
+        banks = [psum.tile([P, 512], F32, name=f"bank{b}") for b in range(8)]
+
+        xs = sb("xs", [P, T], U8)
+        nc.vector.memset(xs[:].bitcast(I32), 0)
+        warm = sb("warm", [P, 2], F32)
+        nc.gpsimd.memset(warm[:], 1.0)
+        warm_out = sb("warm_out", [P, 2], F32)
+        nc.scalar.activation(warm_out[:], warm[:], ACT.Abs_reciprocal_sqrt)
+
+        lists = {}
+
+        def load_list(name, src):
+            lists[name] = sb(name + "_sb", [P, H // 16], U16)
+            nc.sync.dma_start(lists[name][:], src)
+
+        for name, src in (("offs", offs), ("n2", n2), ("n1", n1), ("n4", n4)):
+            load_list(name, src)
+        offs_sb = lists["offs"]
+        xw = sb("xw", [P, T], U32)
+        nc.sync.dma_start(xw[:].bitcast(I32), x_words[0].rearrange("p c r -> p (c r)").bitcast(I32))
+        for q in range(4):
+            nc.scalar.dma_start(xs[32 * q : 32 * q + 4, :].bitcast(I32), x_scales[0][4 * q : 4 * q + 4, :].bitcast(I32))
+        wa_rows = wa.rearrange("(p j) c -> p j c", j=PACK)
+        wa_raw = []
+        for i, (a, b) in enumerate(spans(WA_CHUNKS)):
+            raw = keep.tile([P, PACK, b - a], F32, name=f"wa_raw{i}", tag=f"wa_raw{i}", align_bytes=64)
+            nc.sync.dma_start(raw[:], wa_rows[:, :, a:b])
+            wa_raw.append(raw)
+        load_list("n3", n3)
+        gt_sb = sb("gt_sb", [P, PACK], F32)
+        nc.gpsimd.dma_start(gt_sb[:], gt.rearrange("(p t) o -> p (t o)", t=PACK))
+        w1s = sb("w1s", [P, N], U8)
+        nc.gpsimd.memset(w1s[:].bitcast(I32), 0)
+        w1w = sb("w1w", [P, 2 * N], U8)
+        nc.gpsimd.dma_start(w1w[:].bitcast(I32), w1_words[0].bitcast(I32))
+        for q in range(4):
+            nc.gpsimd.dma_start(w1s[32 * q : 32 * q + 4, :].bitcast(I32), w1_scales[0][4 * q : 4 * q + 4, :].bitcast(I32))
+
+        xs_picked = sb("xs_picked", [P, S], U8)
+        nc.vector.tensor_copy(xs_picked[:], xs[:].indirect(offs_sb[:]))
+        xw_dealt = sb("xw_dealt", [P, PACK, P], U32)
+        nc.vector.tensor_copy(xw_dealt[:].rearrange("p t m -> p m t"), xw[:].indirect(offs_sb[:]))
+        xs_dealt = sb("xs_dealt", [P, PACK, P], U8)
+        nc.vector.tensor_copy(xs_dealt[:], xs_picked[:].rearrange("p (m t) -> p t m", t=PACK))
+
+        y = [sb(f"y{t}", [P, H], F32) for t in range(PACK)]
+        last = len(WA_CHUNKS) - 1
+        for i, (a, b) in enumerate(spans(WA_CHUNKS)):
+            w = b - a
+            grouped = keep.tile([P, w, PACK], BF16, name=f"wa_grouped{i}", tag=f"wa_grouped{i}", align_bytes=64)
+            interleave(nc.vector.tensor_copy if i == last else nc.scalar.copy, grouped[:], wa_raw[i][:])
+            codes = sb(f"wa_codes{i}", [P, w], U32)
+            scales = sb(f"wa_scales{i}", [P, w], U8)
+            nc.vector.quantize_mx(out=codes[:].bitcast(FP8X4), scales=scales[:], in_=grouped[:].rearrange("p c t -> p (c t)"))
+            for t in range(PACK):
+                bank = banks[4 * (i % 2) + t]
+                nc.tensor.matmul_mx(out=bank[:, 0:w], lhsT=xw_dealt[:, t, :].bitcast(FP8X4), lhsT_scale=xs_dealt[:, t, :],
+                                    rhs=codes[:].bitcast(FP8X4), rhs_scale=scales[:], start=True, stop=True)
+                nc.scalar.activation(y[t][:, a:b], bank[:, 0:w], ACT.Copy, scale=gt_sb[:, t : t + 1])
+
+        w1w_dealt = keep.tile([P, PACK, P, 2], U8, name="w1w_dealt", tag="wa_raw1", align_bytes=64)
+        nc.vector.tensor_copy(w1w_dealt[:], w1w[:].rearrange("p (m t b) -> p t m b", t=PACK, b=2))
+        w1s_dealt = keep.tile([P, PACK, P], U8, name="w1s_dealt", tag="wa_grouped1", align_bytes=64)
+        nc.vector.tensor_copy(w1s_dealt[:], w1s[:].rearrange("p (m t) -> p t m", t=PACK))
+
+        h = [sb(f"h{t}", [P, H], F32) for t in range(PACK)]
+        h_plain = sb("h_plain", [P, PACK, H], F32)
+        last = len(Z_CHUNKS) - 1
+        for i, (a, b) in enumerate(spans(Z_CHUNKS)):
+            w = b - a
+            z = sb(f"z{i}", [P, PACK, w], F32)
+            for pair in range(2):
+                tag = f"stage{i - 1}" if pair == 1 and i > 0 else f"second{i}_{pair}"
+                second = keep.tile([P, 2, w], F32, name=f"second{i}_{pair}", tag=tag, align_bytes=64)
+                for u in range(2):
+                    nc.vector.tensor_copy(second[:, u, :], y[2 * pair + u][:].indirect(lists["n2"][:, a // 16 : b // 16]))
+                for u in range(2):
+                    t = 2 * pair + u
+                    nc.vector.tensor_tensor(z[:, t, :], y[t][:].indirect(lists["n1"][:, a // 16 : b // 16]), second[:, u, :], SUB)
+            grouped = keep.tile([P, w, PACK], BF16, name=f"z_grouped{i}", tag=f"stage{i}", align_bytes=64)
+            if i == last:
+                interleave(nc.vector.tensor_copy, grouped[:, :Z_VECTOR_COLS, :], z[:, :, :Z_VECTOR_COLS])
+                interleave(nc.scalar.copy, grouped[:, Z_VECTOR_COLS:, :], z[:, :, Z_VECTOR_COLS:])
+            else:
+                interleave(nc.scalar.copy, grouped[:], z[:])
+            codes = sb(f"z_codes{i}", [P, w], U32)
+            scales = sb(f"z_scales{i}", [P, w], U8)
+            nc.vector.quantize_mx(out=codes[:].bitcast(FP8X4), scales=scales[:], in_=grouped[:].rearrange("p c t -> p (c t)"))
+            for t in range(PACK):
+                bank = banks[4 * (i % 2) + t]
+                nc.tensor.matmul_mx(out=bank[:, 0:w], lhsT=w1w_dealt[:, t].rearrange("p m b -> p (m b)").bitcast(FP4X4), lhsT_scale=w1s_dealt[:, t, :],
+                                    rhs=codes[:].bitcast(FP8X4), rhs_scale=scales[:], start=True, stop=True)
+                nc.scalar.activation(h[t][:, a:b], bank[:, 0:w], ACT.Copy, scale=-1.0)
+            for t in range(PACK):
+                nc.scalar.activation(h_plain[:, t, a:b], banks[4 * (i % 2) + t][:, 0:w], ACT.Copy, scale=-1.0)
+
+        out_rows = out_0.rearrange("(p t) c -> p t c", t=PACK)
+        out_words = out_1[0].rearrange("p c r -> p (c r)").bitcast(I32)
+        out_scales = sb("out_scales", [P, H], U8)
+        chunks = spans(OUT_CHUNKS)
+        last = len(chunks) - 1
+        recips, gaps = {}, {}
+
+        def denominators(i):
+            a, b = chunks[i]
+            w = b - a
+            d = sb(f"d{i}", [P, PACK, w], F32)
+            for t in range(PACK):
+                nc.vector.tensor_tensor(d[:, t, :], h[t][:].indirect(lists["n4"][:, a // 16 : b // 16]), h_plain[:, t, a:b], SUB)
+            mag = sb(f"mag{i}", [P, PACK, w], F32)
+            nc.scalar.activation(mag[:], d[:], ACT.Abs)
+            root = sb(f"root{i}", [P, PACK, w], F32)
+            nc.scalar.activation(root[:], mag[:], ACT.Abs_reciprocal_sqrt, bias=0.5)
+            recips[i] = sb(f"recip{i}", [P, PACK, w], F32)
+            nc.scalar.activation(recips[i][:], root[:], ACT.Square)
+
+        def numerators(i):
+            a, b = chunks[i]
+            gaps[i] = keep.tile([P, PACK, b - a], F32, name=f"gap{i}", tag=f"gap{i % 2}", align_bytes=64)
+            for t in range(PACK):
+                nc.vector.tensor_tensor(gaps[i][:, t, :], h[t][:].indirect(lists["n3"][:, a // 16 : b // 16]), h_plain[:, t, a:b], SUB)
+
+        def finish(i):
+            a, b = chunks[i]
+            w = b - a
+            res = sb(f"res{i}", [P, PACK, w], F32)
+            nc.vector.tensor_tensor(res[:], gaps[i][:], recips[i][:], MULT)
+            nc.sync.dma_start(out_rows[:, :, a:b], res[:])
+            grouped = sb(f"res_grouped{i}", [P, w, PACK], BF16)
+            interleave(nc.vector.tensor_copy if i == last else nc.scalar.copy, grouped[:], res[:])
+            codes = sb(f"res_codes{i}", [P, w], U32)
+            nc.vector.quantize_mx(out=codes[:].bitcast(FP8X4), scales=out_scales[:, a:b], in_=grouped[:].rearrange("p c t -> p (c t)"))
+            nc.sync.dma_start(out_words[:, a:b], codes[:].bitcast(I32))
+
+        denominators(0)
+        numerators(0)
+        denominators(1)
+        denominators(2)
+        numerators(1)
+        finish(0)
+        numerators(2)
+        finish(1)
+        finish(2)
+        for q in range(4):
+            queue = nc.scalar if q % 2 else nc.sync
+            queue.dma_start(out_2[0][4 * q : 4 * q + 4, :].bitcast(I32), out_scales[32 * q : 32 * q + 4, :].bitcast(I32))

@@ -21,7 +21,7 @@ P = 128
 PACK = 4
 WA_CHUNKS = (256, 256)
 Z_CHUNKS = (256, 256)
-Z_VECTOR_COLS = 160
+EARLY_TILES = 2
 OUT_CHUNKS = (256, 128, 128)
 
 
@@ -50,10 +50,17 @@ def tile_picked_tokgapfrac_none_po_kernel(tc, x_words, x_scales, wa, gt, w1_word
 
         xs = sb("xs", [P, T], U8)
         nc.vector.memset(xs[:].bitcast(I32), 0)
-        warm = sb("warm", [P, 2], F32)
-        nc.gpsimd.memset(warm[:], 1.0)
-        warm_out = sb("warm_out", [P, 2], F32)
-        nc.scalar.activation(warm_out[:], warm[:], ACT.Abs_reciprocal_sqrt)
+        warm = keep.tile([P, 2], F32, name="warm", tag="gt", align_bytes=64)
+        nc.vector.memset(warm[:], 1.0)
+        w1s = sb("w1s", [P, N], U8)
+        nc.gpsimd.memset(w1s[:].bitcast(I32), 0)
+        for q in range(4):
+            nc.gpsimd.dma_start(w1s[32 * q : 32 * q + 4, :].bitcast(I32), w1_scales[0][4 * q : 4 * q + 4, :].bitcast(I32))
+
+        w1w = sb("w1w", [P, 2 * N], U8)
+        nc.scalar.dma_start(w1w[:].bitcast(I32), w1_words[0].bitcast(I32))
+        w1w_dealt = sb("w1w_dealt", [P, PACK, P, 2], U8)
+        nc.vector.tensor_copy(w1w_dealt[:], w1w[:].rearrange("p (m t b) -> p t m b", t=PACK, b=2))
 
         lists = {}
 
@@ -64,50 +71,44 @@ def tile_picked_tokgapfrac_none_po_kernel(tc, x_words, x_scales, wa, gt, w1_word
         for name, src in (("offs", offs), ("n2", n2), ("n1", n1), ("n4", n4)):
             load_list(name, src)
         offs_sb = lists["offs"]
-        xw = sb("xw", [P, T], U32)
+        xw = keep.tile([P, T], U32, name="xw", tag="xw", align_bytes=64)
         nc.sync.dma_start(xw[:].bitcast(I32), x_words[0].rearrange("p c r -> p (c r)").bitcast(I32))
         for q in range(4):
             nc.scalar.dma_start(xs[32 * q : 32 * q + 4, :].bitcast(I32), x_scales[0][4 * q : 4 * q + 4, :].bitcast(I32))
+        warm_out = sb("warm_out", [P, 2], F32)
+        nc.scalar.activation(warm_out[:], warm[:], ACT.Abs_reciprocal_sqrt)
         wa_rows = wa.rearrange("(p j) c -> p j c", j=PACK)
         wa_raw = []
         for i, (a, b) in enumerate(spans(WA_CHUNKS)):
-            raw = keep.tile([P, PACK, b - a], F32, name=f"wa_raw{i}", tag=f"wa_raw{i}", align_bytes=64)
+            raw = sb(f"wa_raw{i}", [P, PACK, b - a], F32)
             nc.sync.dma_start(raw[:], wa_rows[:, :, a:b])
             wa_raw.append(raw)
         load_list("n3", n3)
-        gt_sb = sb("gt_sb", [P, PACK], F32)
-        nc.gpsimd.dma_start(gt_sb[:], gt.rearrange("(p t) o -> p (t o)", t=PACK))
-        w1s = sb("w1s", [P, N], U8)
-        nc.gpsimd.memset(w1s[:].bitcast(I32), 0)
-        w1w = sb("w1w", [P, 2 * N], U8)
-        nc.gpsimd.dma_start(w1w[:].bitcast(I32), w1_words[0].bitcast(I32))
-        for q in range(4):
-            nc.gpsimd.dma_start(w1s[32 * q : 32 * q + 4, :].bitcast(I32), w1_scales[0][4 * q : 4 * q + 4, :].bitcast(I32))
+        gt_sb = keep.tile([P, PACK], F32, name="gt_sb", tag="gt", align_bytes=64)
+        nc.sync.dma_start(gt_sb[:], gt.rearrange("(p t) o -> p (t o)", t=PACK))
 
-        xs_picked = sb("xs_picked", [P, S], U8)
-        nc.vector.tensor_copy(xs_picked[:], xs[:].indirect(offs_sb[:]))
         xw_dealt = sb("xw_dealt", [P, PACK, P], U32)
         nc.vector.tensor_copy(xw_dealt[:].rearrange("p t m -> p m t"), xw[:].indirect(offs_sb[:]))
+        xs_picked = keep.tile([P, S], U8, name="xs_picked", tag="xw", align_bytes=64)
+        nc.vector.tensor_copy(xs_picked[:], xs[:].indirect(offs_sb[:]))
         xs_dealt = sb("xs_dealt", [P, PACK, P], U8)
         nc.vector.tensor_copy(xs_dealt[:], xs_picked[:].rearrange("p (m t) -> p t m", t=PACK))
 
         y = [sb(f"y{t}", [P, H], F32) for t in range(PACK)]
-        last = len(WA_CHUNKS) - 1
+        wa_codes = keep.tile([P, H], U32, name="wa_codes", tag="z0", align_bytes=64)
+        wa_scales = sb("wa_scales", [P, H], U8)
         for i, (a, b) in enumerate(spans(WA_CHUNKS)):
-            w = b - a
-            grouped = keep.tile([P, w, PACK], BF16, name=f"wa_grouped{i}", tag=f"wa_grouped{i}", align_bytes=64)
-            interleave(nc.vector.tensor_copy if i == last else nc.scalar.copy, grouped[:], wa_raw[i][:])
-            codes = sb(f"wa_codes{i}", [P, w], U32)
-            scales = sb(f"wa_scales{i}", [P, w], U8)
-            nc.vector.quantize_mx(out=codes[:].bitcast(FP8X4), scales=scales[:], in_=grouped[:].rearrange("p c t -> p (c t)"))
-            for t in range(PACK):
-                bank = banks[4 * (i % 2) + t]
-                nc.tensor.matmul_mx(out=bank[:, 0:w], lhsT=xw_dealt[:, t, :].bitcast(FP8X4), lhsT_scale=xs_dealt[:, t, :],
-                                    rhs=codes[:].bitcast(FP8X4), rhs_scale=scales[:], start=True, stop=True)
-                nc.scalar.activation(y[t][:, a:b], bank[:, 0:w], ACT.Copy, scale=gt_sb[:, t : t + 1])
+            grouped = keep.tile([P, b - a, PACK], BF16, name=f"wa_grouped{i}", tag=f"wa_grouped{i}", align_bytes=64)
+            interleave(nc.scalar.copy, grouped[:], wa_raw[i][:])
+            nc.vector.quantize_mx(out=wa_codes[:, a:b].bitcast(FP8X4), scales=wa_scales[:, a:b], in_=grouped[:].rearrange("p c t -> p (c t)"))
+        for t in range(PACK):
+            pieces = spans(WA_CHUNKS) if t < EARLY_TILES else [(0, H)]
+            for a, b in pieces:
+                bank = banks[4 + t] if b == H else banks[t]
+                nc.tensor.matmul_mx(out=bank[:, 0 : b - a], lhsT=xw_dealt[:, t, :].bitcast(FP8X4), lhsT_scale=xs_dealt[:, t, :],
+                                    rhs=wa_codes[:, a:b].bitcast(FP8X4), rhs_scale=wa_scales[:, a:b], start=True, stop=True)
+                nc.scalar.activation(y[t][:, a:b], bank[:, 0 : b - a], ACT.Copy, scale=gt_sb[:, t : t + 1])
 
-        w1w_dealt = keep.tile([P, PACK, P, 2], U8, name="w1w_dealt", tag="wa_raw1", align_bytes=64)
-        nc.vector.tensor_copy(w1w_dealt[:], w1w[:].rearrange("p (m t b) -> p t m b", t=PACK, b=2))
         w1s_dealt = keep.tile([P, PACK, P], U8, name="w1s_dealt", tag="wa_grouped1", align_bytes=64)
         nc.vector.tensor_copy(w1s_dealt[:], w1s[:].rearrange("p (m t) -> p t m", t=PACK))
 
@@ -116,21 +117,18 @@ def tile_picked_tokgapfrac_none_po_kernel(tc, x_words, x_scales, wa, gt, w1_word
         last = len(Z_CHUNKS) - 1
         for i, (a, b) in enumerate(spans(Z_CHUNKS)):
             w = b - a
-            z = sb(f"z{i}", [P, PACK, w], F32)
-            for pair in range(2):
-                tag = f"stage{i - 1}" if pair == 1 and i > 0 else f"second{i}_{pair}"
-                second = keep.tile([P, 2, w], F32, name=f"second{i}_{pair}", tag=tag, align_bytes=64)
-                for u in range(2):
-                    nc.vector.tensor_copy(second[:, u, :], y[2 * pair + u][:].indirect(lists["n2"][:, a // 16 : b // 16]))
-                for u in range(2):
-                    t = 2 * pair + u
-                    nc.vector.tensor_tensor(z[:, t, :], y[t][:].indirect(lists["n1"][:, a // 16 : b // 16]), second[:, u, :], SUB)
-            grouped = keep.tile([P, w, PACK], BF16, name=f"z_grouped{i}", tag=f"stage{i}", align_bytes=64)
-            if i == last:
-                interleave(nc.vector.tensor_copy, grouped[:, :Z_VECTOR_COLS, :], z[:, :, :Z_VECTOR_COLS])
-                interleave(nc.scalar.copy, grouped[:, Z_VECTOR_COLS:, :], z[:, :, Z_VECTOR_COLS:])
-            else:
-                interleave(nc.scalar.copy, grouped[:], z[:])
+            z = keep.tile([P, PACK, w], F32, name=f"z{i}", tag=f"z{i}", align_bytes=64)
+            second = []
+            for step in range(PACK + 1):
+                if step < PACK:
+                    tag = "z_grouped0" if (i, step) == (1, 2) else f"second{step}"
+                    second.append(keep.tile([P, w], F32, name=f"second{i}_{step}", tag=tag, align_bytes=64))
+                    nc.vector.tensor_copy(second[step][:], y[step][:].indirect(lists["n2"][:, a // 16 : b // 16]))
+                if step > 0:
+                    t = step - 1
+                    nc.vector.tensor_tensor(z[:, t, :], y[t][:].indirect(lists["n1"][:, a // 16 : b // 16]), second[t][:], SUB)
+            grouped = keep.tile([P, w, PACK], BF16, name=f"z_grouped{i}", tag=f"z_grouped{i}", align_bytes=64)
+            interleave(nc.vector.tensor_copy if i == last else nc.scalar.copy, grouped[:], z[:])
             codes = sb(f"z_codes{i}", [P, w], U32)
             scales = sb(f"z_scales{i}", [P, w], U8)
             nc.vector.quantize_mx(out=codes[:].bitcast(FP8X4), scales=scales[:], in_=grouped[:].rearrange("p c t -> p (c t)"))
@@ -181,9 +179,9 @@ def tile_picked_tokgapfrac_none_po_kernel(tc, x_words, x_scales, wa, gt, w1_word
             nc.sync.dma_start(out_words[:, a:b], codes[:].bitcast(I32))
 
         denominators(0)
-        numerators(0)
         denominators(1)
         denominators(2)
+        numerators(0)
         numerators(1)
         finish(0)
         numerators(2)

@@ -50,15 +50,14 @@ def tile_picked_tokgapfrac_none_po_kernel(tc, x_words, x_scales, wa, gt, w1_word
 
         xs = sb("xs", [P, T], U8)
         nc.vector.memset(xs[:].bitcast(I32), 0)
-        warm = keep.tile([P, 2], F32, name="warm", tag="gt", align_bytes=64)
+        warm = keep.tile([P, 2], F32, name="warm", tag="wa_raw0", align_bytes=64)
         nc.vector.memset(warm[:], 1.0)
-        w1s = sb("w1s", [P, N], U8)
-        nc.gpsimd.memset(w1s[:].bitcast(I32), 0)
-        for q in range(4):
-            nc.gpsimd.dma_start(w1s[32 * q : 32 * q + 4, :].bitcast(I32), w1_scales[0][4 * q : 4 * q + 4, :].bitcast(I32))
-
-        w1w = sb("w1w", [P, 2 * N], U8)
+        gt_sb = sb("gt_sb", [P, PACK], F32)
+        nc.scalar.dma_start(gt_sb[:], gt.rearrange("(p t) o -> p (t o)", t=PACK))
+        w1w = keep.tile([P, 2 * N], U8, name="w1w", tag="w1_raw", align_bytes=64)
         nc.scalar.dma_start(w1w[:].bitcast(I32), w1_words[0].bitcast(I32))
+        warm_out = keep.tile([P, 2], F32, name="warm_out", tag="wa_raw1", align_bytes=64)
+        nc.scalar.activation(warm_out[:], warm[:], ACT.Abs_reciprocal_sqrt)
         w1w_dealt = sb("w1w_dealt", [P, PACK, P, 2], U8)
         nc.vector.tensor_copy(w1w_dealt[:], w1w[:].rearrange("p (m t b) -> p t m b", t=PACK, b=2))
 
@@ -73,19 +72,20 @@ def tile_picked_tokgapfrac_none_po_kernel(tc, x_words, x_scales, wa, gt, w1_word
         offs_sb = lists["offs"]
         xw = keep.tile([P, T], U32, name="xw", tag="xw", align_bytes=64)
         nc.sync.dma_start(xw[:].bitcast(I32), x_words[0].rearrange("p c r -> p (c r)").bitcast(I32))
+        load_list("n3", n3)
         for q in range(4):
-            nc.scalar.dma_start(xs[32 * q : 32 * q + 4, :].bitcast(I32), x_scales[0][4 * q : 4 * q + 4, :].bitcast(I32))
-        warm_out = sb("warm_out", [P, 2], F32)
-        nc.scalar.activation(warm_out[:], warm[:], ACT.Abs_reciprocal_sqrt)
+            nc.sync.dma_start(xs[32 * q : 32 * q + 4, :].bitcast(I32), x_scales[0][4 * q : 4 * q + 4, :].bitcast(I32))
         wa_rows = wa.rearrange("(p j) c -> p j c", j=PACK)
         wa_raw = []
         for i, (a, b) in enumerate(spans(WA_CHUNKS)):
-            raw = sb(f"wa_raw{i}", [P, PACK, b - a], F32)
+            raw = keep.tile([P, PACK, b - a], F32, name=f"wa_raw{i}", tag=f"wa_raw{i}", align_bytes=64)
             nc.sync.dma_start(raw[:], wa_rows[:, :, a:b])
             wa_raw.append(raw)
-        load_list("n3", n3)
-        gt_sb = keep.tile([P, PACK], F32, name="gt_sb", tag="gt", align_bytes=64)
-        nc.sync.dma_start(gt_sb[:], gt.rearrange("(p t) o -> p (t o)", t=PACK))
+
+        w1s = keep.tile([P, N], U8, name="w1s", tag="w1_raw", align_bytes=64)
+        nc.vector.memset(w1s[:].bitcast(I32), 0)
+        for q in range(4):
+            nc.sync.dma_start(w1s[32 * q : 32 * q + 4, :].bitcast(I32), w1_scales[0][4 * q : 4 * q + 4, :].bitcast(I32))
 
         xw_dealt = sb("xw_dealt", [P, PACK, P], U32)
         nc.vector.tensor_copy(xw_dealt[:].rearrange("p t m -> p m t"), xw[:].indirect(offs_sb[:]))

from contextlib import ExitStack

import concourse.mybir as mybir

K, T, S, N, H = 512, 2048, 512, 512, 512
FLOPS = 2 * K * S * H + 2 * S * N * H

F32 = mybir.dt.float32
BF16 = mybir.dt.bfloat16
I32 = mybir.dt.int32
U32 = mybir.dt.uint32
U16 = mybir.dt.uint16
U8 = mybir.dt.uint8
FP8X4 = mybir.dt.float8_e4m3fn_x4
FP4X4 = mybir.dt.float4_e2m1fn_x4
ACT = mybir.ActivationFunctionType
SUB = mybir.AluOpType.subtract
MULT = mybir.AluOpType.mult

P = 128
PACK = 4
WA_CHUNKS = (256, 256)
Z_CHUNKS = (256, 256)
EARLY_TILES = 2
OUT_CHUNKS = (256, 128, 128)


def spans(widths):
    out, at = [], 0
    for w in widths:
        out.append((at, at + w))
        at = at + w
    return out


def interleave(copy, dst, src):
    copy(dst.rearrange("p (c i) t -> p c t i", i=4), src.rearrange("p t (c i) -> p c t i", i=4))


def tile_picked_tokgapfrac_none_po_kernel(tc, x_words, x_scales, wa, gt, w1_words, w1_scales, offs, n1, n2, n3, n4, out_0, out_1, out_2):
    nc = tc.nc
    with ExitStack() as ctx:
        keep = ctx.enter_context(tc.tile_pool(name="keep", bufs=1))
        psum = ctx.enter_context(tc.psum_pool(name="psum", bufs=1))

        def sb(name, shape, dtype):
            return keep.tile(shape, dtype, name=name, align_bytes=64)

        banks = [psum.tile([P, 512], F32, name=f"bank{b}") for b in range(8)]

        xs = sb("xs", [P, T], U8)
        nc.vector.memset(xs[:].bitcast(I32), 0)
        warm = keep.tile([P, 2], F32, name="warm", tag="wa_raw0", align_bytes=64)
        nc.vector.memset(warm[:], 1.0)
        gt_sb = sb("gt_sb", [P, PACK], F32)
        nc.scalar.dma_start(gt_sb[:], gt.rearrange("(p t) o -> p (t o)", t=PACK))
        w1w = keep.tile([P, 2 * N], U8, name="w1w", tag="w1_raw", align_bytes=64)
        nc.scalar.dma_start(w1w[:].bitcast(I32), w1_words[0].bitcast(I32))
        warm_out = keep.tile([P, 2], F32, name="warm_out", tag="wa_raw1", align_bytes=64)
        nc.scalar.activation(warm_out[:], warm[:], ACT.Abs_reciprocal_sqrt)
        w1w_dealt = sb("w1w_dealt", [P, PACK, P, 2], U8)
        nc.vector.tensor_copy(w1w_dealt[:], w1w[:].rearrange("p (m t b) -> p t m b", t=PACK, b=2))

        lists = {}

        def load_list(name, src):
            lists[name] = sb(name + "_sb", [P, H // 16], U16)
            nc.sync.dma_start(lists[name][:], src)

        for name, src in (("offs", offs), ("n2", n2), ("n1", n1), ("n4", n4)):
            load_list(name, src)
        offs_sb = lists["offs"]
        xw = keep.tile([P, T], U32, name="xw", tag="xw", align_bytes=64)
        nc.sync.dma_start(xw[:].bitcast(I32), x_words[0].rearrange("p c r -> p (c r)").bitcast(I32))
        load_list("n3", n3)
        for q in range(4):
            nc.sync.dma_start(xs[32 * q : 32 * q + 4, :].bitcast(I32), x_scales[0][4 * q : 4 * q + 4, :].bitcast(I32))
        wa_rows = wa.rearrange("(p j) c -> p j c", j=PACK)
        wa_raw = []
        for i, (a, b) in enumerate(spans(WA_CHUNKS)):
            raw = keep.tile([P, PACK, b - a], F32, name=f"wa_raw{i}", tag=f"wa_raw{i}", align_bytes=64)
            nc.sync.dma_start(raw[:], wa_rows[:, :, a:b])
            wa_raw.append(raw)

        w1s = keep.tile([P, N], U8, name="w1s", tag="w1_raw", align_bytes=64)
        nc.vector.memset(w1s[:].bitcast(I32), 0)
        for q in range(4):
            nc.sync.dma_start(w1s[32 * q : 32 * q + 4, :].bitcast(I32), w1_scales[0][4 * q : 4 * q + 4, :].bitcast(I32))

        xw_dealt = sb("xw_dealt", [P, PACK, P], U32)
        nc.vector.tensor_copy(xw_dealt[:].rearrange("p t m -> p m t"), xw[:].indirect(offs_sb[:]))
        xs_picked = keep.tile([P, S], U8, name="xs_picked", tag="xw", align_bytes=64)
        nc.vector.tensor_copy(xs_picked[:], xs[:].indirect(offs_sb[:]))
        xs_dealt = sb("xs_dealt", [P, PACK, P], U8)
        nc.vector.tensor_copy(xs_dealt[:], xs_picked[:].rearrange("p (m t) -> p t m", t=PACK))

        y = [sb(f"y{t}", [P, H], F32) for t in range(PACK)]
        wa_codes = keep.tile([P, H], U32, name="wa_codes", tag="z0", align_bytes=64)
        wa_scales = sb("wa_scales", [P, H], U8)
        for i, (a, b) in enumerate(spans(WA_CHUNKS)):
            grouped = keep.tile([P, b - a, PACK], BF16, name=f"wa_grouped{i}", tag=f"wa_grouped{i}", align_bytes=64)
            interleave(nc.scalar.copy, grouped[:], wa_raw[i][:])
            nc.vector.quantize_mx(out=wa_codes[:, a:b].bitcast(FP8X4), scales=wa_scales[:, a:b], in_=grouped[:].rearrange("p c t -> p (c t)"))
        for t in range(PACK):
            pieces = spans(WA_CHUNKS) if t < EARLY_TILES else [(0, H)]
            for a, b in pieces:
                bank = banks[4 + t] if b == H else banks[t]
                nc.tensor.matmul_mx(out=bank[:, 0 : b - a], lhsT=xw_dealt[:, t, :].bitcast(FP8X4), lhsT_scale=xs_dealt[:, t, :],
                                    rhs=wa_codes[:, a:b].bitcast(FP8X4), rhs_scale=wa_scales[:, a:b], start=True, stop=True)
                nc.scalar.activation(y[t][:, a:b], bank[:, 0 : b - a], ACT.Copy, scale=gt_sb[:, t : t + 1])

        w1s_dealt = keep.tile([P, PACK, P], U8, name="w1s_dealt", tag="wa_grouped1", align_bytes=64)
        nc.vector.tensor_copy(w1s_dealt[:], w1s[:].rearrange("p (m t) -> p t m", t=PACK))

        h = [sb(f"h{t}", [P, H], F32) for t in range(PACK)]
        h_plain = sb("h_plain", [P, PACK, H], F32)
        last = len(Z_CHUNKS) - 1
        for i, (a, b) in enumerate(spans(Z_CHUNKS)):
            w = b - a
            z = keep.tile([P, PACK, w], F32, name=f"z{i}", tag=f"z{i}", align_bytes=64)
            second = []
            for step in range(PACK + 1):
                if step < PACK:
                    tag = "z_grouped0" if (i, step) == (1, 2) else f"second{step}"
                    second.append(keep.tile([P, w], F32, name=f"second{i}_{step}", tag=tag, align_bytes=64))
                    nc.vector.tensor_copy(second[step][:], y[step][:].indirect(lists["n2"][:, a // 16 : b // 16]))
                if step > 0:
                    t = step - 1
                    nc.vector.tensor_tensor(z[:, t, :], y[t][:].indirect(lists["n1"][:, a // 16 : b // 16]), second[t][:], SUB)
            grouped = keep.tile([P, w, PACK], BF16, name=f"z_grouped{i}", tag=f"z_grouped{i}", align_bytes=64)
            interleave(nc.vector.tensor_copy if i == last else nc.scalar.copy, grouped[:], z[:])
            codes = sb(f"z_codes{i}", [P, w], U32)
            scales = sb(f"z_scales{i}", [P, w], U8)
            nc.vector.quantize_mx(out=codes[:].bitcast(FP8X4), scales=scales[:], in_=grouped[:].rearrange("p c t -> p (c t)"))
            for t in range(PACK):
                bank = banks[4 * (i % 2) + t]
                nc.tensor.matmul_mx(out=bank[:, 0:w], lhsT=w1w_dealt[:, t].rearrange("p m b -> p (m b)").bitcast(FP4X4), lhsT_scale=w1s_dealt[:, t, :],
                                    rhs=codes[:].bitcast(FP8X4), rhs_scale=scales[:], start=True, stop=True)
                nc.scalar.activation(h[t][:, a:b], bank[:, 0:w], ACT.Copy, scale=-1.0)
            for t in range(PACK):
                nc.scalar.activation(h_plain[:, t, a:b], banks[4 * (i % 2) + t][:, 0:w], ACT.Copy, scale=-1.0)

        out_rows = out_0.rearrange("(p t) c -> p t c", t=PACK)
        out_words = out_1[0].rearrange("p c r -> p (c r)").bitcast(I32)
        out_scales = sb("out_scales", [P, H], U8)
        chunks = spans(OUT_CHUNKS)
        last = len(chunks) - 1
        recips, gaps = {}, {}

        def denominators(i):
            a, b = chunks[i]
            w = b - a
            d = sb(f"d{i}", [P, PACK, w], F32)
            for t in range(PACK):
                nc.vector.tensor_tensor(d[:, t, :], h[t][:].indirect(lists["n4"][:, a // 16 : b // 16]), h_plain[:, t, a:b], SUB)
            mag = sb(f"mag{i}", [P, PACK, w], F32)
            nc.scalar.activation(mag[:], d[:], ACT.Abs)
            root = sb(f"root{i}", [P, PACK, w], F32)
            nc.scalar.activation(root[:], mag[:], ACT.Abs_reciprocal_sqrt, bias=0.5)
            recips[i] = sb(f"recip{i}", [P, PACK, w], F32)
            nc.scalar.activation(recips[i][:], root[:], ACT.Square)

        def numerators(i):
            a, b = chunks[i]
            gaps[i] = keep.tile([P, PACK, b - a], F32, name=f"gap{i}", tag=f"gap{i % 2}", align_bytes=64)
            for t in range(PACK):
                nc.vector.tensor_tensor(gaps[i][:, t, :], h[t][:].indirect(lists["n3"][:, a // 16 : b // 16]), h_plain[:, t, a:b], SUB)

        def finish(i):
            a, b = chunks[i]
            w = b - a
            res = sb(f"res{i}", [P, PACK, w], F32)
            nc.vector.tensor_tensor(res[:], gaps[i][:], recips[i][:], MULT)
            nc.sync.dma_start(out_rows[:, :, a:b], res[:])
            grouped = sb(f"res_grouped{i}", [P, w, PACK], BF16)
            interleave(nc.vector.tensor_copy if i == last else nc.scalar.copy, grouped[:], res[:])
            codes = sb(f"res_codes{i}", [P, w], U32)
            nc.vector.quantize_mx(out=codes[:].bitcast(FP8X4), scales=out_scales[:, a:b], in_=grouped[:].rearrange("p c t -> p (c t)"))
            nc.sync.dma_start(out_words[:, a:b], codes[:].bitcast(I32))

        denominators(0)
        denominators(1)
        denominators(2)
        numerators(0)
        numerators(1)
        finish(0)
        numerators(2)
        finish(1)
        finish(2)
        for q in range(4):
            queue = nc.scalar if q % 2 else nc.sync
            queue.dma_start(out_2[0][4 * q : 4 * q + 4, :].bitcast(I32), out_scales[32 * q : 32 * q + 4, :].bitcast(I32))
